import numpy as np
import ml_dtypes


def mxq(x, axis, fmt="e4m3"):
    dtype, down = {"e4m3": (ml_dtypes.float8_e4m3fn, 7), "e5m2": (ml_dtypes.float8_e5m2, 14)}[fmt]
    v = np.moveaxis(np.asarray(x, np.float32).astype(ml_dtypes.bfloat16).astype(np.float64), axis, -1)
    blocks = v.reshape(v.shape[:-1] + (-1, 32))
    amax = np.abs(blocks).max(-1, keepdims=True)
    byte = np.maximum(np.where(amax > 0, np.frexp(amax)[1] - 1 + 127, 0) - down, 1)
    scale = np.exp2(byte - 127.0)
    codes = (blocks / scale).astype(np.float32).astype(dtype).astype(np.float64)
    return np.moveaxis((codes * scale).reshape(v.shape), -1, axis)


WIDE = False


def mx_kscale(k):
    if not WIDE:
        return np.ones(k)
    levels = np.array([10, -10, 5, -5, 0])
    if k % 512:
        return np.exp2(np.random.permutation(np.resize(levels, k // 32))).repeat(32)
    a = np.empty((k // 512, 16))
    for p in range(k // 512):
        a[p, :8] = np.random.permutation(np.resize(levels, 8))
        for g in range(8):
            far = levels[np.abs(levels - a[p, g]) >= 10]
            a[p, g + 8] = far[np.random.randint(len(far))]
    return np.exp2(a.ravel()).repeat(32)


def f64(x):
    return np.asarray(x).astype(np.float64)


def striped(idx):
    return np.tile(idx.reshape(-1, 16).T, (8, 1)).astype(np.uint16)


def unstriped(offs):
    return offs[:16].T.reshape(-1).astype(np.int64)


def striped8(idx):
    return np.concatenate([x.reshape(-1, 16).T for x in idx]).astype(np.uint16)


def runs(offs, k):
    lists = np.stack([offs[16 * r : 16 * r + 16].T.reshape(-1) for r in range(8)]).astype(np.int64)
    return lists[np.arange(k) % 512 // 64]


def pack_weight(w):
    k, n = w.shape
    w = f64(np.asarray(w, np.float32).astype(ml_dtypes.bfloat16)).reshape(k // 32, 32, n)
    amax = np.abs(w).max(1)
    byte = np.clip(np.where(amax > 0, np.frexp(amax)[1] - 1 + 127 - 7, 1), 1, 254)
    scaled = (w * np.exp2(127.0 - byte)[:, None, :]).reshape(k, n).astype(np.float32)
    words = np.ascontiguousarray(scaled.reshape(k // 512, 128, 4, n).transpose(0, 1, 3, 2)).astype(ml_dtypes.float8_e4m3fn).view(np.uint8)
    return words, np.ascontiguousarray(byte.astype(np.uint8).reshape(k // 512, 16, n))


def unpack_weight(words, scales):
    g, p, n, _ = words.shape
    vals = np.ascontiguousarray(words).view(ml_dtypes.float8_e4m3fn).astype(np.float64) * np.repeat(np.exp2(scales.astype(np.float64) - 127.0), 8, axis=1)[..., None]
    return vals.transpose(0, 1, 3, 2).reshape(g * 512, n)


def sigmoid(v):
    return 1.0 / (1.0 + np.exp(-np.maximum(v, -700.0)))


K, T, S, N, G, H = 512, 1024, 512, 512, 2048, 512


def setup_inputs():
    n = np.random.standard_normal
    s = mx_kscale(K)[:, None]
    u = mx_kscale(S)
    packed_xT = pack_weight(n((K, T)) * s)
    packed_dT = pack_weight(n((K, G)) / s)
    return {
        "x_words": packed_xT[0],
        "x_scales": packed_xT[1],
        "d_words": packed_dT[0],
        "d_scales": packed_dT[1],
        "gn": (np.random.uniform(0.5, 1.5, (H, 1)) * u[:, None]).astype(np.float32),
        "w1": (n((H, N)) / np.sqrt(2 * H) / u[:, None]).astype(np.float32),
        "w2": (n((K, N)) / np.sqrt(2 * K) / s).astype(np.float32),
        "sl": np.random.uniform(1.5, 2.5, (N, 1)).astype(np.float32),
        "lo": np.random.uniform(-1.2, -0.4, (N, 1)).astype(np.float32),
        "hi": np.random.uniform(0.4, 1.2, (N, 1)).astype(np.float32),
        "offs": striped(np.random.permutation(T)[:S]),
        "k1": striped8(np.random.randint(0, G, (8, H))),
        "n1": striped(np.random.permutation(S)),
        "n2": striped(np.random.permutation(S)),
        "two": striped(np.random.permutation(T)[:S]),
        "n3": striped(np.random.permutation(S)),
    }


def reference(x_words, x_scales, d_words, d_scales, gn, w1, w2, sl, lo, hi, offs, k1, n1, n2, two, n3):
    d_k1 = unpack_weight(d_words, d_scales)[np.arange(K)[:, None], runs(k1, K)]
    xq = unpack_weight(x_words, x_scales)[:, unstriped(offs)]
    h = 0.0625 * (d_k1.T @ xq)
    z = f64(gn) * (h[:, unstriped(n1)] / (np.abs(h) + np.abs(h[:, unstriped(n2)]) + 0.5))
    x_two = unpack_weight(x_words, x_scales)[:, unstriped(two)]
    h2 = mxq(f64(w1), 0, "e4m3").T @ mxq(z, 0, "e4m3") + mxq(f64(w2), 0, "e4m3").T @ x_two
    sg = sigmoid(f64(sl) * (h2[:, unstriped(n3)] - f64(lo)))
    sg2 = sigmoid(f64(sl) * (h2[:, unstriped(n3)] - f64(hi)))
    return h2 * (sg - sg2)

@@ -1,0 +1,243 @@
+from contextlib import ExitStack
+
+import concourse.mybir as mybir
+
+F32 = mybir.dt.float32
+BF16 = mybir.dt.bfloat16
+I32 = mybir.dt.int32
+U32 = mybir.dt.uint32
+U16 = mybir.dt.uint16
+U8 = mybir.dt.uint8
+FP8X4 = mybir.dt.float8_e4m3fn_x4
+ACT = mybir.ActivationFunctionType
+ALU = mybir.AluOpType
+
+P = 128
+K, T, S, N, G, H = 512, 1024, 512, 512, 2048, 512
+PACK = 4
+TILES = 4
+HALF = S // 2
+FLOPS = 3 * 2 * 512 * 512 * 512
+
+
+def tile_picked_pqmixnorm2ebd_none_p_kernel(
+    tc, x_words, x_scales, d_words, d_scales, gn, w1, w2, sl, lo, hi, offs, k1, n1, n2, two, n3, out
+):
+    nc = tc.nc
+    with ExitStack() as ctx:
+        sb = ctx.enter_context(tc.tile_pool(name="sb", bufs=1))
+        reuse = ctx.enter_context(tc.tile_pool(name="reuse", bufs=1))
+        ps = ctx.enter_context(tc.psum_pool(name="ps", bufs=1))
+
+        def load_list(src, name):
+            t = sb.tile([P, S // 16], U16, name=name)
+            nc.sync.dma_start(t[:], src)
+            return t
+
+        def entries(lst, span):
+            return lst[:, span.start // 16 : span.stop // 16]
+
+        def cols(hf):
+            return slice(hf * HALF, (hf + 1) * HALF)
+
+        def blk(t):
+            return slice(t * P, (t + 1) * P)
+
+        k1_t = load_list(k1, "k1_t")
+        d_bytes = sb.tile([P, G], U8, name="d_bytes", align_bytes=64)
+        nc.sync.dma_start(
+            d_bytes[:].bitcast(I32),
+            d_scales[0].bitcast(I32).unsqueeze(1).to_broadcast([16, 8, G // 4]),
+        )
+        offs_t = load_list(offs, "offs_t")
+        x_bytes = sb.tile([P, T], U8, name="x_bytes", align_bytes=64)
+        for q in range(4):
+            nc.sync.dma_start(
+                x_bytes[32 * q : 32 * q + 32, :].bitcast(I32),
+                x_scales[0, 4 * q : 4 * q + 4, :].bitcast(I32).unsqueeze(0).to_broadcast([8, 4, T // 4]),
+            )
+        d_tab = reuse.tile([P, G], I32, name="d_tab", align_bytes=64, offset=6080)
+        nc.sync.dma_start(d_tab[:], d_words[0].rearrange("p n t -> p (n t)").bitcast(I32))
+        two_t = load_list(two, "two_t")
+        x_tab = reuse.tile([P, T], I32, name="x_tab", align_bytes=64, offset=24960)
+        nc.sync.dma_start(x_tab[:], x_words[0].rearrange("p n t -> p (n t)").bitcast(I32))
+        n2_t = load_list(n2, "n2_t")
+        n1_t = load_list(n1, "n1_t")
+        n3_t = load_list(n3, "n3_t")
+        gain = sb.tile([P, TILES], F32, name="gain")
+        nc.gpsimd.dma_start(gain[:], gn.rearrange("(p t) o -> p (t o)", t=PACK))
+        h2 = [sb.tile([P, 2 * S], F32, name="h2_%d" % m) for m in range(TILES)]
+        for m in range(TILES):
+            nc.gpsimd.memset(h2[m][:, S:], 0.0)
+
+        d_sg = reuse.tile([P, H], U8, name="d_sg", align_bytes=64, offset=22464)
+        nc.vector.tensor_copy(d_sg[:], d_bytes[:].indirect(k1_t[:]))
+        d_sc = sb.tile([P, H], U8, name="d_sc", tag="d_sc", align_bytes=64)
+        nc.vector.tensor_copy(
+            d_sc[:].rearrange("p (t m) -> p m t", t=PACK), d_sg[:].rearrange("p (m t) -> p m t", t=PACK)
+        )
+        for c in range(1, 4):
+            nc.sync.dma_start(d_sc[c:P:32, :].bitcast(I32), d_sc[8 * c : P : 32, :].bitcast(I32))
+        w2_rows = w2.rearrange("(p j) n -> p j n", j=PACK)
+        w1_rows = w1.rearrange("(p j) n -> p j n", j=PACK)
+        w2_head = reuse.tile([P, PACK, P], F32, name="w2_head", align_bytes=64, offset=20480)
+        nc.sync.dma_start(w2_head[:], w2_rows[:, :, 0:P])
+        w1_head = reuse.tile([P, PACK, P], F32, name="w1_head", align_bytes=64, offset=22912)
+        nc.sync.dma_start(w1_head[:], w1_rows[:, :, 0:P])
+        xq_s = sb.tile([P, S], U8, name="xq_s", align_bytes=64)
+        nc.vector.tensor_copy(xq_s[:], x_bytes[:].indirect(offs_t[:]))
+        d_wg = sb.tile([P, H], U32, name="d_wg", align_bytes=64)
+        nc.vector.tensor_copy(d_wg[:], d_tab[:].bitcast(U32).indirect(k1_t[:]))
+        d_w = sb.tile([P, H], U32, name="d_w", align_bytes=64)
+        nc.vector.tensor_copy(
+            d_w[:].rearrange("p (t m) -> p m t", t=PACK), d_wg[:].rearrange("p (m t) -> p m t", t=PACK)
+        )
+        xq_w = reuse.tile([P, S], U32, name="xq_w", align_bytes=64, offset=6144)
+        nc.vector.tensor_copy(xq_w[:], x_tab[:].bitcast(U32).indirect(offs_t[:]))
+        w2_rest = reuse.tile([P, PACK, N - P], F32, name="w2_rest", align_bytes=64, offset=0)
+        nc.sync.dma_start(w2_rest[:], w2_rows[:, :, P:N])
+        w1_rest = reuse.tile([P, PACK, N - P], F32, name="w1_rest", align_bytes=64, offset=14208)
+        nc.sync.dma_start(w1_rest[:], w1_rows[:, :, P:N])
+
+        def round_weight(copy, raw, name, tag):
+            grp = sb.tile([P, P, PACK], BF16, name=name + "_b", tag=tag, align_bytes=64)
+            copy(grp[:].rearrange("p (c i) t -> p c t i", i=4), raw.rearrange("p t (c i) -> p c t i", i=4))
+            return grp
+
+        def quantise_weight(grp, name):
+            wq = sb.tile([P, P], U32, name=name + "_w", align_bytes=64)
+            ws = sb.tile([P, P], U8, name=name + "_s", align_bytes=64)
+            nc.vector.quantize_mx(out=wq[:].bitcast(FP8X4), scales=ws[:], in_=grp[:].rearrange("p c t -> p (c t)"))
+            return wq, ws
+
+        w2_b0 = round_weight(nc.scalar.copy, w2_head[:], "w2_0", "w2_0")
+        w1_b0 = round_weight(nc.scalar.copy, w1_head[:], "w1_0", "w1_0")
+
+        h_ps = []
+        for t in range(TILES):
+            acc = ps.tile([P, S], F32, name="h_ps%d" % t, tag="a%d" % t)
+            nc.tensor.matmul_mx(
+                out=acc[:], lhsT=d_w[:, blk(t)].bitcast(FP8X4), lhsT_scale=d_sc[:, blk(t)],
+                rhs=xq_w[:].bitcast(FP8X4), rhs_scale=xq_s[:], start=True, stop=True,
+            )
+            h_ps.append(acc)
+
+        x2_w = reuse.tile([P, S], U32, name="x2_w", align_bytes=64, offset=8192)
+        nc.vector.tensor_copy(x2_w[:], x_tab[:].bitcast(U32).indirect(two_t[:]))
+        x2_s = reuse.tile([P, S], U8, name="x2_s", align_bytes=64, offset=24960)
+        nc.vector.tensor_copy(x2_s[:], x_bytes[:].indirect(two_t[:]))
+        w2q0 = quantise_weight(w2_b0, "w2_0")
+        w1q0 = quantise_weight(w1_b0, "w1_0")
+
+        prm = sb.tile([P, 3, 8], F32, name="prm", tag="d_sc", align_bytes=64)
+        with nc.allow_non_contiguous_dma(reason="one value a partition and tile"):
+            for i, vec in enumerate((sl, lo, hi)):
+                nc.sync.dma_start(prm[:, i, 0:TILES], vec.rearrange("(t p) o -> p (t o)", t=TILES))
+        nsl = sb.tile([P, 4], F32, name="nsl")
+        nc.gpsimd.tensor_scalar(nsl[:], prm[:, 0, 0:TILES], -1.0, 0.0, ALU.mult, ALU.add)
+        b_lo = sb.tile([P, 4], F32, name="b_lo")
+        nc.gpsimd.tensor_tensor(b_lo[:], nsl[:], prm[:, 1, 0:TILES], ALU.mult)
+        b_hi = sb.tile([P, 4], F32, name="b_hi")
+        nc.gpsimd.tensor_tensor(b_hi[:], nsl[:], prm[:, 2, 0:TILES], ALU.mult)
+
+        size = [reuse.tile([P, S], F32, name="size0", align_bytes=64, offset=21504)]
+        size.extend(sb.tile([P, S], F32, name="size%d" % t) for t in range(1, TILES))
+        num = [sb.tile([P, S], F32, name="num%d" % t) for t in range(TILES)]
+        far = [
+            [sb.tile([P, HALF], F32, name="far%d_%d" % (hf, t), tag="far%d_%d" % (hf, t), align_bytes=64) for t in range(TILES)]
+            for hf in range(2)
+        ]
+        den = [
+            [sb.tile([P, HALF], F32, name="den%d_%d" % (hf, t), tag="den%d_%d" % (hf, t), align_bytes=64) for t in range(TILES)]
+            for hf in range(2)
+        ]
+        root = sb.tile([P, 2, TILES, HALF], F32, name="root")
+        part = [sb.tile([P, TILES, HALF], F32, name="part%d" % hf, tag="part%d" % hf, align_bytes=64) for hf in range(2)]
+        z_w = sb.tile([P, S], U32, name="z_w", align_bytes=64)
+        z_s = sb.tile([P, S], U8, name="z_s", align_bytes=64)
+
+        def windows(t):
+            nc.scalar.activation(size[t][:], h_ps[t][:], ACT.Abs)
+            if t in (1, 2, 3):
+                nc.vector.tensor_scalar(num[t][:], h_ps[t][:], gain[:, t : t + 1], None, ALU.mult)
+            else:
+                nc.scalar.activation(num[t][:], h_ps[t][:], ACT.Copy, scale=gain[:, t : t + 1])
+
+        def fetch_far(hf, t):
+            nc.scalar.activation(far[hf][t][:], size[t][:].indirect(entries(n2_t, cols(hf))), ACT.Copy)
+            nc.vector.tensor_tensor(den[hf][t][:], far[hf][t][:], size[t][:, cols(hf)], ALU.add)
+
+        def finish(hf, t):
+            picked = num[t][:].indirect(entries(n1_t, cols(hf)))
+            if (hf, t) in ((1, 2), (1, 3)):
+                near = sb.tile([P, HALF], F32, name="near%d_%d" % (hf, t))
+                nc.scalar.activation(near[:], picked, ACT.Copy)
+                picked = near[:]
+            nc.scalar.activation(root[:, hf, t, :], den[hf][t][:], ACT.Abs_reciprocal_sqrt, bias=8.0)
+            nc.vector.tensor_tensor(part[hf][:, t, :], picked, root[:, hf, t, :], ALU.mult)
+
+        def quantise_z(hf):
+            z_b = sb.tile([P, HALF, PACK], BF16, name="z_b%d" % hf, tag="z_b%d" % hf, align_bytes=64)
+            nc.vector.tensor_tensor(
+                z_b[:].rearrange("p (c i) t -> p c t i", i=4),
+                part[hf][:].rearrange("p t (c i) -> p c t i", i=4),
+                root[:, hf].rearrange("p t (c i) -> p c t i", i=4),
+                ALU.mult,
+            )
+            nc.vector.quantize_mx(
+                out=z_w[:, cols(hf)].bitcast(FP8X4), scales=z_s[:, cols(hf)], in_=z_b[:].rearrange("p c t -> p (c t)")
+            )
+
+        def second_product(m, w1q, w2q, span, tag):
+            acc = ps.tile([P, span.stop - span.start], F32, name="h2_ps_" + tag, tag=tag)
+            nc.tensor.matmul_mx(
+                out=acc[:], lhsT=w2q[0][:].bitcast(FP8X4), lhsT_scale=w2q[1][:],
+                rhs=x2_w[:, span].bitcast(FP8X4), rhs_scale=x2_s[:, span], start=True, stop=False,
+            )
+            nc.tensor.matmul_mx(
+                out=acc[:], lhsT=w1q[0][:].bitcast(FP8X4), lhsT_scale=w1q[1][:],
+                rhs=z_w[:, span].bitcast(FP8X4), rhs_scale=z_s[:, span], start=False, stop=True,
+            )
+            nc.vector.tensor_copy(h2[m][:, span], acc[:])
+
+        steps = [(hf, t) for hf in range(2) for t in range(TILES)]
+        for i, (hf, t) in enumerate(steps):
+            if hf == 0:
+                windows(t)
+            fetch_far(hf, t)
+            if i > 0:
+                finish(*steps[i - 1])
+            if i == TILES:
+                quantise_z(0)
+                second_product(0, w1q0, w2q0, cols(0), "b0")
+        finish(*steps[-1])
+        quantise_z(1)
+        second_product(0, w1q0, w2q0, cols(1), "b1")
+
+        def gates(m, spans):
+            res = sb.tile([P, S], F32, name="res%d" % m)
+            sg = sb.tile([P, S], F32, name="sg%d" % m)
+            sg2 = sb.tile([P, S], F32, name="sgh%d" % m)
+            dif = sb.tile([P, S], F32, name="dif%d" % m)
+            for span in spans:
+                window = h2[m][:].indirect(entries(n3_t, span))
+                slope = prm[:, 0, m : m + 1]
+                nc.scalar.activation(sg[:, span], window, ACT.Sigmoid, bias=b_lo[:, m : m + 1], scale=slope)
+                nc.scalar.activation(sg2[:, span], window, ACT.Sigmoid, bias=b_hi[:, m : m + 1], scale=slope)
+                nc.vector.tensor_tensor(dif[:, span], sg[:, span], sg2[:, span], ALU.subtract)
+                nc.vector.tensor_tensor(res[:, span], dif[:, span], h2[m][:, span], ALU.mult)
+                nc.sync.dma_start(out[blk(m), span], res[:, span])
+
+        whole = slice(0, S)
+        for m in range(TILES):
+            if m + 1 < TILES:
+                if m == 0:
+                    copy, tags = nc.scalar.copy, ("den1_3", "far1_3")
+                else:
+                    copy, tags = nc.vector.tensor_copy, ("part1", "z_b1")
+                w2_b = round_weight(copy, w2_rest[:, :, blk(m)], "w2_%d" % (m + 1), tags[0])
+                w1_b = round_weight(copy, w1_rest[:, :, blk(m)], "w1_%d" % (m + 1), tags[1])
+                w2q = quantise_weight(w2_b, "w2_%d" % (m + 1))
+                w1q = quantise_weight(w1_b, "w1_%d" % (m + 1))
+                second_product(m + 1, w1q, w2q, whole, "a%d" % m)
+            gates(m, [whole] if m + 1 < TILES else [cols(0), cols(1)])

@@ -43,6 +43,9 @@ def tile_picked_pqmixnorm2ebd_none_p_kernel(
         def blk(t):
             return slice(t * P, (t + 1) * P)
 
+        warm = sb.tile([P, 3], F32, name="warm")
+        nc.vector.memset(warm[:, 0:1], 1.0)
+        nc.scalar.activation(warm[:, 1:2], warm[:, 0:1], ACT.Abs_reciprocal_sqrt)
         k1_t = load_list(k1, "k1_t")
         d_bytes = sb.tile([P, G], U8, name="d_bytes", align_bytes=64)
         nc.sync.dma_start(
@@ -211,6 +214,7 @@ def tile_picked_pqmixnorm2ebd_none_p_kernel(
                 quantise_z(0)
                 second_product(0, w1q0, w2q0, cols(0), "b0")
         finish(*steps[-1])
+        nc.scalar.activation(warm[:, 2:3], root[:, 1, TILES - 1, 0:1], ACT.Sigmoid)
         quantise_z(1)
         second_product(0, w1q0, w2q0, cols(1), "b1")
 

@@ -69,8 +69,8 @@ def tile_picked_pqmixnorm2ebd_none_p_kernel(
         n3_t = load_list(n3, "n3_t")
         gain = sb.tile([P, TILES], F32, name="gain")
         nc.gpsimd.dma_start(gain[:], gn.rearrange("(p t) o -> p (t o)", t=PACK))
-        h2 = [sb.tile([P, 2 * S], F32, name="h2_%d" % m) for m in range(TILES)]
-        for m in range(TILES):
+        h2 = [sb.tile([P, 2 * S if m + 1 < TILES else S], F32, name="h2_%d" % m) for m in range(TILES)]
+        for m in range(TILES - 1):
             nc.gpsimd.memset(h2[m][:, S:], 0.0)
 
         d_sg = reuse.tile([P, H], U8, name="d_sg", align_bytes=64, offset=22464)
@@ -146,77 +146,84 @@ def tile_picked_pqmixnorm2ebd_none_p_kernel(
         size = [reuse.tile([P, S], F32, name="size0", align_bytes=64, offset=21504)]
         size.extend(sb.tile([P, S], F32, name="size%d" % t) for t in range(1, TILES))
         num = [sb.tile([P, S], F32, name="num%d" % t) for t in range(TILES)]
-        far = [
-            [sb.tile([P, HALF], F32, name="far%d_%d" % (hf, t), tag="far%d_%d" % (hf, t), align_bytes=64) for t in range(TILES)]
-            for hf in range(2)
+        spans = (slice(0, 384), slice(384, S))
+        widths = [sp.stop - sp.start for sp in spans]
+        left = [
+            sb.tile([P, TILES, widths[pt]], F32, name="left%d" % pt, tag="left%d" % pt, align_bytes=64) for pt in range(2)
         ]
-        den = [
-            [sb.tile([P, HALF], F32, name="den%d_%d" % (hf, t), tag="den%d_%d" % (hf, t), align_bytes=64) for t in range(TILES)]
-            for hf in range(2)
+        right = [
+            sb.tile([P, TILES, widths[pt]], F32, name="right%d" % pt, tag="right%d" % pt, align_bytes=64) for pt in range(2)
         ]
-        root = sb.tile([P, 2, TILES, HALF], F32, name="root")
-        part = [sb.tile([P, TILES, HALF], F32, name="part%d" % hf, tag="part%d" % hf, align_bytes=64) for hf in range(2)]
+        den = {}
         z_w = sb.tile([P, S], U32, name="z_w", align_bytes=64)
         z_s = sb.tile([P, S], U8, name="z_s", align_bytes=64)
 
         def windows(t):
             nc.scalar.activation(size[t][:], h_ps[t][:], ACT.Abs)
-            if t in (1, 2, 3):
+            if t in (0, 1, 2, 3):
                 nc.vector.tensor_scalar(num[t][:], h_ps[t][:], gain[:, t : t + 1], None, ALU.mult)
             else:
                 nc.scalar.activation(num[t][:], h_ps[t][:], ACT.Copy, scale=gain[:, t : t + 1])
 
-        def fetch_far(hf, t):
-            nc.scalar.activation(far[hf][t][:], size[t][:].indirect(entries(n2_t, cols(hf))), ACT.Copy)
-            nc.vector.tensor_tensor(den[hf][t][:], far[hf][t][:], size[t][:, cols(hf)], ALU.add)
+        def fetch_far(pt, t):
+            far = sb.tile([P, widths[pt]], F32, name="far%d_%d" % (pt, t))
+            nc.scalar.activation(far[:], size[t][:].indirect(entries(n2_t, spans[pt])), ACT.Copy)
+            den[pt, t] = sb.tile([P, widths[pt]], F32, name="den%d_%d" % (pt, t), tag="den%d_%d" % (pt, t), align_bytes=64)
+            nc.vector.tensor_tensor(den[pt, t][:], far[:], size[t][:, spans[pt]], ALU.add)
 
-        def finish(hf, t):
-            picked = num[t][:].indirect(entries(n1_t, cols(hf)))
-            if (hf, t) in ((1, 2), (1, 3)):
-                near = sb.tile([P, HALF], F32, name="near%d_%d" % (hf, t))
-                nc.scalar.activation(near[:], picked, ACT.Copy)
-                picked = near[:]
-            nc.scalar.activation(root[:, hf, t, :], den[hf][t][:], ACT.Abs_reciprocal_sqrt, bias=8.0)
-            nc.vector.tensor_tensor(part[hf][:, t, :], picked, root[:, hf, t, :], ALU.mult)
+        def finish(pt, t):
+            picked = num[t][:].indirect(entries(n1_t, spans[pt]))
+            if (pt, t) in ((1, 0), (1, 1), (1, 2), (1, 3)):
+                nc.scalar.activation(left[pt][:, t, :], picked, ACT.Copy)
+                root = sb.tile([P, widths[pt]], F32, name="root%d_%d" % (pt, t), tag="root%d_%d" % (pt, t), align_bytes=64)
+                nc.scalar.activation(root[:], den[pt, t][:], ACT.Abs_reciprocal_sqrt, bias=8.0)
+                nc.scalar.activation(right[pt][:, t, :], root[:], ACT.Square)
+            else:
+                nc.scalar.activation(right[pt][:, t, :], den[pt, t][:], ACT.Abs_reciprocal_sqrt, bias=8.0)
+                nc.vector.tensor_tensor(left[pt][:, t, :], picked, right[pt][:, t, :], ALU.mult)
 
-        def quantise_z(hf):
-            z_b = sb.tile([P, HALF, PACK], BF16, name="z_b%d" % hf, tag="z_b%d" % hf, align_bytes=64)
+        def quantise_z(pt):
+            z_b = sb.tile([P, widths[pt], PACK], BF16, name="z_b%d" % pt, tag="z_b%d" % pt, align_bytes=64)
             nc.vector.tensor_tensor(
                 z_b[:].rearrange("p (c i) t -> p c t i", i=4),
-                part[hf][:].rearrange("p t (c i) -> p c t i", i=4),
-                root[:, hf].rearrange("p t (c i) -> p c t i", i=4),
+                left[pt][:].rearrange("p t (c i) -> p c t i", i=4),
+                right[pt][:].rearrange("p t (c i) -> p c t i", i=4),
                 ALU.mult,
             )
             nc.vector.quantize_mx(
-                out=z_w[:, cols(hf)].bitcast(FP8X4), scales=z_s[:, cols(hf)], in_=z_b[:].rearrange("p c t -> p (c t)")
+                out=z_w[:, spans[pt]].bitcast(FP8X4), scales=z_s[:, spans[pt]], in_=z_b[:].rearrange("p c t -> p (c t)")
             )
 
-        def second_product(m, w1q, w2q, span, tag):
+        def second_product(m, w1q, w2q, span, tag, copy_out):
             acc = ps.tile([P, span.stop - span.start], F32, name="h2_ps_" + tag, tag=tag)
-            nc.tensor.matmul_mx(
-                out=acc[:], lhsT=w2q[0][:].bitcast(FP8X4), lhsT_scale=w2q[1][:],
-                rhs=x2_w[:, span].bitcast(FP8X4), rhs_scale=x2_s[:, span], start=True, stop=False,
-            )
-            nc.tensor.matmul_mx(
-                out=acc[:], lhsT=w1q[0][:].bitcast(FP8X4), lhsT_scale=w1q[1][:],
-                rhs=z_w[:, span].bitcast(FP8X4), rhs_scale=z_s[:, span], start=False, stop=True,
-            )
-            nc.vector.tensor_copy(h2[m][:, span], acc[:])
+            cuts = [span.start, span.stop] if span.stop - span.start != 384 else [span.start, span.start + 256, span.stop]
+            for c0, c1 in zip(cuts, cuts[1:]):
+                dst = acc[:, c0 - span.start : c1 - span.start]
+                nc.tensor.matmul_mx(
+                    out=dst, lhsT=w2q[0][:].bitcast(FP8X4), lhsT_scale=w2q[1][:],
+                    rhs=x2_w[:, c0:c1].bitcast(FP8X4), rhs_scale=x2_s[:, c0:c1], start=True, stop=False,
+                )
+                nc.tensor.matmul_mx(
+                    out=dst, lhsT=w1q[0][:].bitcast(FP8X4), lhsT_scale=w1q[1][:],
+                    rhs=z_w[:, c0:c1].bitcast(FP8X4), rhs_scale=z_s[:, c0:c1], start=False, stop=True,
+                )
+            copy_out(h2[m][:, span], acc[:])
 
-        steps = [(hf, t) for hf in range(2) for t in range(TILES)]
-        for i, (hf, t) in enumerate(steps):
-            if hf == 0:
-                windows(t)
-            fetch_far(hf, t)
-            if i > 0:
-                finish(*steps[i - 1])
-            if i == TILES:
-                quantise_z(0)
-                second_product(0, w1q0, w2q0, cols(0), "b0")
-        finish(*steps[-1])
-        nc.scalar.activation(warm[:, 2:3], root[:, 1, TILES - 1, 0:1], ACT.Sigmoid)
-        quantise_z(1)
-        second_product(0, w1q0, w2q0, cols(1), "b1")
+        LAG = 2
+        steps = [(pt, t) for pt in range(2) for t in range(TILES)]
+        for i in range(len(steps) + LAG):
+            if i < TILES:
+                windows(i)
+            if i < len(steps):
+                fetch_far(*steps[i])
+            if i >= LAG:
+                pt, t = steps[i - LAG]
+                finish(pt, t)
+                if t == TILES - 1:
+                    if pt == 1:
+                        nc.scalar.activation(warm[:, 2:3], right[1][:, TILES - 1, 0:1], ACT.Sigmoid)
+                    quantise_z(pt)
+                    second_product(0, w1q0, w2q0, spans[pt], "b%d" % pt, (nc.vector.tensor_copy, nc.vector.tensor_copy)[pt])
 
         def gates(m, spans):
             res = sb.tile([P, S], F32, name="res%d" % m)
@@ -235,13 +242,13 @@ def tile_picked_pqmixnorm2ebd_none_p_kernel(
         whole = slice(0, S)
         for m in range(TILES):
             if m + 1 < TILES:
-                if m == 0:
-                    copy, tags = nc.scalar.copy, ("den1_3", "far1_3")
+                if m < 1:
+                    copy, tags = nc.scalar.copy, ("w2_%d" % (m + 1), "w1_%d" % (m + 1))
                 else:
-                    copy, tags = nc.vector.tensor_copy, ("part1", "z_b1")
+                    copy, tags = nc.vector.tensor_copy, ("left1", "z_b1")
                 w2_b = round_weight(copy, w2_rest[:, :, blk(m)], "w2_%d" % (m + 1), tags[0])
                 w1_b = round_weight(copy, w1_rest[:, :, blk(m)], "w1_%d" % (m + 1), tags[1])
                 w2q = quantise_weight(w2_b, "w2_%d" % (m + 1))
                 w1q = quantise_weight(w1_b, "w1_%d" % (m + 1))
-                second_product(m + 1, w1q, w2q, whole, "a%d" % m)
-            gates(m, [whole] if m + 1 < TILES else [cols(0), cols(1)])
+                second_product(m + 1, w1q, w2q, whole, "a%d" % m, nc.vector.tensor_copy)
+            gates(m, [whole] if m + 1 < TILES else [slice(0, 256), slice(256, 384), slice(384, S)])

@@ -70,8 +70,6 @@ def tile_picked_pqmixnorm2ebd_none_p_kernel(
         gain = sb.tile([P, TILES], F32, name="gain")
         nc.gpsimd.dma_start(gain[:], gn.rearrange("(p t) o -> p (t o)", t=PACK))
         h2 = [sb.tile([P, 2 * S if m + 1 < TILES else S], F32, name="h2_%d" % m) for m in range(TILES)]
-        for m in range(TILES - 1):
-            nc.gpsimd.memset(h2[m][:, S:], 0.0)
 
         d_sg = reuse.tile([P, H], U8, name="d_sg", align_bytes=64, offset=22464)
         nc.vector.tensor_copy(d_sg[:], d_bytes[:].indirect(k1_t[:]))
@@ -155,6 +153,7 @@ def tile_picked_pqmixnorm2ebd_none_p_kernel(
             sb.tile([P, TILES, widths[pt]], F32, name="right%d" % pt, tag="right%d" % pt, align_bytes=64) for pt in range(2)
         ]
         den = {}
+        last_far = sb.tile([P, S], F32, name="last_far")
         z_w = sb.tile([P, S], U32, name="z_w", align_bytes=64)
         z_s = sb.tile([P, S], U8, name="z_s", align_bytes=64)
 
@@ -166,10 +165,13 @@ def tile_picked_pqmixnorm2ebd_none_p_kernel(
                 nc.scalar.activation(num[t][:], h_ps[t][:], ACT.Copy, scale=gain[:, t : t + 1])
 
         def fetch_far(pt, t):
-            far = sb.tile([P, widths[pt]], F32, name="far%d_%d" % (pt, t))
-            nc.scalar.activation(far[:], size[t][:].indirect(entries(n2_t, spans[pt])), ACT.Copy)
+            if t + 1 < TILES:
+                far = h2[t][:, S + spans[pt].start : S + spans[pt].stop]
+            else:
+                far = last_far[:, spans[pt]]
+            nc.scalar.activation(far, size[t][:].indirect(entries(n2_t, spans[pt])), ACT.Copy)
             den[pt, t] = sb.tile([P, widths[pt]], F32, name="den%d_%d" % (pt, t), tag="den%d_%d" % (pt, t), align_bytes=64)
-            nc.vector.tensor_tensor(den[pt, t][:], far[:], size[t][:, spans[pt]], ALU.add)
+            nc.vector.tensor_tensor(den[pt, t][:], far, size[t][:, spans[pt]], ALU.add)
 
         def finish(pt, t):
             picked = num[t][:].indirect(entries(n1_t, spans[pt]))
@@ -223,7 +225,7 @@ def tile_picked_pqmixnorm2ebd_none_p_kernel(
                     if pt == 1:
                         nc.scalar.activation(warm[:, 2:3], right[1][:, TILES - 1, 0:1], ACT.Sigmoid)
                     quantise_z(pt)
-                    second_product(0, w1q0, w2q0, spans[pt], "b%d" % pt, (nc.vector.tensor_copy, nc.vector.tensor_copy)[pt])
+                    second_product(0, w1q0, w2q0, spans[pt], "b%d" % pt, (nc.scalar.copy, nc.vector.tensor_copy)[pt])
 
         def gates(m, spans):
             res = sb.tile([P, S], F32, name="res%d" % m)
@@ -243,7 +245,7 @@ def tile_picked_pqmixnorm2ebd_none_p_kernel(
         for m in range(TILES):
             if m + 1 < TILES:
                 if m < 1:
-                    copy, tags = nc.scalar.copy, ("w2_%d" % (m + 1), "w1_%d" % (m + 1))
+                    copy, tags = nc.scalar.copy, ("den0_1", "den0_2")
                 else:
                     copy, tags = nc.vector.tensor_copy, ("left1", "z_b1")
                 w2_b = round_weight(copy, w2_rest[:, :, blk(m)], "w2_%d" % (m + 1), tags[0])

@@ -13,11 +13,28 @@ ACT = mybir.ActivationFunctionType
 ALU = mybir.AluOpType
 
 P = 128
-K, T, S, N, G, H = 512, 1024, 512, 512, 2048, 512
+T, S, N, G, H = 1024, 512, 512, 2048, 512
 PACK = 4
 TILES = 4
-HALF = S // 2
 FLOPS = 3 * 2 * 512 * 512 * 512
+
+PARTS = (slice(0, 384), slice(384, S))
+PART_CUTS = ((0, 256, 384), (384, S))
+ALL_CUTS = (0, S)
+LAST_PIECES = (slice(0, 256), slice(256, 384), slice(384, S))
+LAG = 2
+
+OVERLAP = 64
+AT_W2_REST = 0
+AT_D_TAB = AT_W2_REST + PACK * (N - P) * 4 - OVERLAP
+AT_XQ_W = AT_D_TAB + OVERLAP
+AT_X2_W = AT_XQ_W + S * 4
+AT_W1_REST = AT_D_TAB + G * 4 - OVERLAP
+AT_W2_HEAD = AT_W1_REST + PACK * (N - P) * 4 + 2 * OVERLAP
+AT_D_SG = AT_W2_HEAD + PACK * P * 4 - OVERLAP
+AT_W1_HEAD = AT_D_SG + H - OVERLAP
+AT_SIZE0 = AT_W2_HEAD + S * 2
+AT_X_TAB = AT_W1_HEAD + PACK * P * 4
 
 
 def tile_picked_pqmixnorm2ebd_none_p_kernel(
@@ -30,15 +47,12 @@ def tile_picked_pqmixnorm2ebd_none_p_kernel(
         ps = ctx.enter_context(tc.psum_pool(name="ps", bufs=1))
 
         def load_list(src, name):
-            t = sb.tile([P, S // 16], U16, name=name)
-            nc.sync.dma_start(t[:], src)
-            return t
+            lst = sb.tile([P, S // 16], U16, name=name)
+            nc.sync.dma_start(lst[:], src)
+            return lst
 
         def entries(lst, span):
             return lst[:, span.start // 16 : span.stop // 16]
-
-        def cols(hf):
-            return slice(hf * HALF, (hf + 1) * HALF)
 
         def blk(t):
             return slice(t * P, (t + 1) * P)
@@ -46,12 +60,13 @@ def tile_picked_pqmixnorm2ebd_none_p_kernel(
         warm = sb.tile([P, 3], F32, name="warm")
         nc.vector.memset(warm[:, 0:1], 1.0)
         nc.scalar.activation(warm[:, 1:2], warm[:, 0:1], ACT.Abs_reciprocal_sqrt)
-        k1_t = load_list(k1, "k1_t")
+
         d_bytes = sb.tile([P, G], U8, name="d_bytes", align_bytes=64)
         nc.sync.dma_start(
             d_bytes[:].bitcast(I32),
             d_scales[0].bitcast(I32).unsqueeze(1).to_broadcast([16, 8, G // 4]),
         )
+        k1_t = load_list(k1, "k1_t")
         offs_t = load_list(offs, "offs_t")
         x_bytes = sb.tile([P, T], U8, name="x_bytes", align_bytes=64)
         for q in range(4):
@@ -59,10 +74,10 @@ def tile_picked_pqmixnorm2ebd_none_p_kernel(
                 x_bytes[32 * q : 32 * q + 32, :].bitcast(I32),
                 x_scales[0, 4 * q : 4 * q + 4, :].bitcast(I32).unsqueeze(0).to_broadcast([8, 4, T // 4]),
             )
-        d_tab = reuse.tile([P, G], I32, name="d_tab", align_bytes=64, offset=6080)
+        d_tab = reuse.tile([P, G], I32, name="d_tab", align_bytes=64, offset=AT_D_TAB)
         nc.sync.dma_start(d_tab[:], d_words[0].rearrange("p n t -> p (n t)").bitcast(I32))
         two_t = load_list(two, "two_t")
-        x_tab = reuse.tile([P, T], I32, name="x_tab", align_bytes=64, offset=24960)
+        x_tab = reuse.tile([P, T], I32, name="x_tab", align_bytes=64, offset=AT_X_TAB)
         nc.sync.dma_start(x_tab[:], x_words[0].rearrange("p n t -> p (n t)").bitcast(I32))
         n2_t = load_list(n2, "n2_t")
         n1_t = load_list(n1, "n1_t")
@@ -71,7 +86,7 @@ def tile_picked_pqmixnorm2ebd_none_p_kernel(
         nc.gpsimd.dma_start(gain[:], gn.rearrange("(p t) o -> p (t o)", t=PACK))
         h2 = [sb.tile([P, 2 * S if m + 1 < TILES else S], F32, name="h2_%d" % m) for m in range(TILES)]
 
-        d_sg = reuse.tile([P, H], U8, name="d_sg", align_bytes=64, offset=22464)
+        d_sg = reuse.tile([P, H], U8, name="d_sg", align_bytes=64, offset=AT_D_SG)
         nc.vector.tensor_copy(d_sg[:], d_bytes[:].indirect(k1_t[:]))
         d_sc = sb.tile([P, H], U8, name="d_sc", tag="d_sc", align_bytes=64)
         nc.vector.tensor_copy(
@@ -81,9 +96,9 @@ def tile_picked_pqmixnorm2ebd_none_p_kernel(
             nc.sync.dma_start(d_sc[c:P:32, :].bitcast(I32), d_sc[8 * c : P : 32, :].bitcast(I32))
         w2_rows = w2.rearrange("(p j) n -> p j n", j=PACK)
         w1_rows = w1.rearrange("(p j) n -> p j n", j=PACK)
-        w2_head = reuse.tile([P, PACK, P], F32, name="w2_head", align_bytes=64, offset=20480)
+        w2_head = reuse.tile([P, PACK, P], F32, name="w2_head", align_bytes=64, offset=AT_W2_HEAD)
         nc.sync.dma_start(w2_head[:], w2_rows[:, :, 0:P])
-        w1_head = reuse.tile([P, PACK, P], F32, name="w1_head", align_bytes=64, offset=22912)
+        w1_head = reuse.tile([P, PACK, P], F32, name="w1_head", align_bytes=64, offset=AT_W1_HEAD)
         nc.sync.dma_start(w1_head[:], w1_rows[:, :, 0:P])
         xq_s = sb.tile([P, S], U8, name="xq_s", align_bytes=64)
         nc.vector.tensor_copy(xq_s[:], x_bytes[:].indirect(offs_t[:]))
@@ -93,11 +108,11 @@ def tile_picked_pqmixnorm2ebd_none_p_kernel(
         nc.vector.tensor_copy(
             d_w[:].rearrange("p (t m) -> p m t", t=PACK), d_wg[:].rearrange("p (m t) -> p m t", t=PACK)
         )
-        xq_w = reuse.tile([P, S], U32, name="xq_w", align_bytes=64, offset=6144)
+        xq_w = reuse.tile([P, S], U32, name="xq_w", align_bytes=64, offset=AT_XQ_W)
         nc.vector.tensor_copy(xq_w[:], x_tab[:].bitcast(U32).indirect(offs_t[:]))
-        w2_rest = reuse.tile([P, PACK, N - P], F32, name="w2_rest", align_bytes=64, offset=0)
+        w2_rest = reuse.tile([P, PACK, N - P], F32, name="w2_rest", align_bytes=64, offset=AT_W2_REST)
         nc.sync.dma_start(w2_rest[:], w2_rows[:, :, P:N])
-        w1_rest = reuse.tile([P, PACK, N - P], F32, name="w1_rest", align_bytes=64, offset=14208)
+        w1_rest = reuse.tile([P, PACK, N - P], F32, name="w1_rest", align_bytes=64, offset=AT_W1_REST)
         nc.sync.dma_start(w1_rest[:], w1_rows[:, :, P:N])
 
         def round_weight(copy, raw, name, tag):
@@ -105,8 +120,8 @@ def tile_picked_pqmixnorm2ebd_none_p_kernel(
             copy(grp[:].rearrange("p (c i) t -> p c t i", i=4), raw.rearrange("p t (c i) -> p c t i", i=4))
             return grp
 
-        def quantise_weight(grp, name):
-            wq = sb.tile([P, P], U32, name=name + "_w", align_bytes=64)
+        def quantise_weight(grp, name, tag):
+            wq = sb.tile([P, P], U32, name=name + "_w", tag=tag, align_bytes=64)
             ws = sb.tile([P, P], U8, name=name + "_s", align_bytes=64)
             nc.vector.quantize_mx(out=wq[:].bitcast(FP8X4), scales=ws[:], in_=grp[:].rearrange("p c t -> p (c t)"))
             return wq, ws
@@ -114,38 +129,37 @@ def tile_picked_pqmixnorm2ebd_none_p_kernel(
         w2_b0 = round_weight(nc.scalar.copy, w2_head[:], "w2_0", "w2_0")
         w1_b0 = round_weight(nc.scalar.copy, w1_head[:], "w1_0", "w1_0")
 
-        h_ps = []
+        s_ps = []
         for t in range(TILES):
-            acc = ps.tile([P, S], F32, name="h_ps%d" % t, tag="a%d" % t)
+            acc = ps.tile([P, S], F32, name="s_ps%d" % t, tag="a%d" % t)
             nc.tensor.matmul_mx(
                 out=acc[:], lhsT=d_w[:, blk(t)].bitcast(FP8X4), lhsT_scale=d_sc[:, blk(t)],
                 rhs=xq_w[:].bitcast(FP8X4), rhs_scale=xq_s[:], start=True, stop=True,
             )
-            h_ps.append(acc)
+            s_ps.append(acc)
 
-        x2_w = reuse.tile([P, S], U32, name="x2_w", align_bytes=64, offset=8192)
+        x2_w = reuse.tile([P, S], U32, name="x2_w", align_bytes=64, offset=AT_X2_W)
         nc.vector.tensor_copy(x2_w[:], x_tab[:].bitcast(U32).indirect(two_t[:]))
-        x2_s = reuse.tile([P, S], U8, name="x2_s", align_bytes=64, offset=24960)
+        x2_s = reuse.tile([P, S], U8, name="x2_s", align_bytes=64, offset=AT_X_TAB)
         nc.vector.tensor_copy(x2_s[:], x_bytes[:].indirect(two_t[:]))
-        w2q0 = quantise_weight(w2_b0, "w2_0")
-        w1q0 = quantise_weight(w1_b0, "w1_0")
+        w2q0 = quantise_weight(w2_b0, "w2_0", "w2_0_w")
+        w1q0 = quantise_weight(w1_b0, "w1_0", "w1_0_w")
 
         prm = sb.tile([P, 3, 8], F32, name="prm", tag="d_sc", align_bytes=64)
         with nc.allow_non_contiguous_dma(reason="one value a partition and tile"):
             for i, vec in enumerate((sl, lo, hi)):
                 nc.sync.dma_start(prm[:, i, 0:TILES], vec.rearrange("(t p) o -> p (t o)", t=TILES))
-        nsl = sb.tile([P, 4], F32, name="nsl")
-        nc.gpsimd.tensor_scalar(nsl[:], prm[:, 0, 0:TILES], -1.0, 0.0, ALU.mult, ALU.add)
-        b_lo = sb.tile([P, 4], F32, name="b_lo")
-        nc.gpsimd.tensor_tensor(b_lo[:], nsl[:], prm[:, 1, 0:TILES], ALU.mult)
-        b_hi = sb.tile([P, 4], F32, name="b_hi")
-        nc.gpsimd.tensor_tensor(b_hi[:], nsl[:], prm[:, 2, 0:TILES], ALU.mult)
+        neg_sl = sb.tile([P, TILES], F32, name="neg_sl")
+        nc.gpsimd.tensor_scalar(neg_sl[:], prm[:, 0, 0:TILES], -1.0, 0.0, ALU.mult, ALU.add)
+        b_lo = sb.tile([P, TILES], F32, name="b_lo")
+        nc.gpsimd.tensor_tensor(b_lo[:], neg_sl[:], prm[:, 1, 0:TILES], ALU.mult)
+        b_hi = sb.tile([P, TILES], F32, name="b_hi")
+        nc.gpsimd.tensor_tensor(b_hi[:], neg_sl[:], prm[:, 2, 0:TILES], ALU.mult)
 
-        size = [reuse.tile([P, S], F32, name="size0", align_bytes=64, offset=21504)]
+        size = [reuse.tile([P, S], F32, name="size0", align_bytes=64, offset=AT_SIZE0)]
         size.extend(sb.tile([P, S], F32, name="size%d" % t) for t in range(1, TILES))
         num = [sb.tile([P, S], F32, name="num%d" % t) for t in range(TILES)]
-        spans = (slice(0, 384), slice(384, S))
-        widths = [sp.stop - sp.start for sp in spans]
+        widths = [span.stop - span.start for span in PARTS]
         left = [
             sb.tile([P, TILES, widths[pt]], F32, name="left%d" % pt, tag="left%d" % pt, align_bytes=64) for pt in range(2)
         ]
@@ -157,25 +171,22 @@ def tile_picked_pqmixnorm2ebd_none_p_kernel(
         z_w = sb.tile([P, S], U32, name="z_w", align_bytes=64)
         z_s = sb.tile([P, S], U8, name="z_s", align_bytes=64)
 
-        def windows(t):
-            nc.scalar.activation(size[t][:], h_ps[t][:], ACT.Abs)
-            if t in (0, 1, 2, 3):
-                nc.vector.tensor_scalar(num[t][:], h_ps[t][:], gain[:, t : t + 1], None, ALU.mult)
-            else:
-                nc.scalar.activation(num[t][:], h_ps[t][:], ACT.Copy, scale=gain[:, t : t + 1])
+        def leave_psum(t):
+            nc.scalar.activation(size[t][:], s_ps[t][:], ACT.Abs)
+            nc.vector.tensor_scalar(num[t][:], s_ps[t][:], gain[:, t : t + 1], None, ALU.mult)
 
-        def fetch_far(pt, t):
+        def denominator(pt, t):
             if t + 1 < TILES:
-                far = h2[t][:, S + spans[pt].start : S + spans[pt].stop]
+                far = h2[t][:, S + PARTS[pt].start : S + PARTS[pt].stop]
             else:
-                far = last_far[:, spans[pt]]
-            nc.scalar.activation(far, size[t][:].indirect(entries(n2_t, spans[pt])), ACT.Copy)
+                far = last_far[:, PARTS[pt]]
+            nc.scalar.activation(far, size[t][:].indirect(entries(n2_t, PARTS[pt])), ACT.Copy)
             den[pt, t] = sb.tile([P, widths[pt]], F32, name="den%d_%d" % (pt, t), tag="den%d_%d" % (pt, t), align_bytes=64)
-            nc.vector.tensor_tensor(den[pt, t][:], far, size[t][:, spans[pt]], ALU.add)
+            nc.vector.tensor_tensor(den[pt, t][:], far, size[t][:, PARTS[pt]], ALU.add)
 
-        def finish(pt, t):
-            picked = num[t][:].indirect(entries(n1_t, spans[pt]))
-            if (pt, t) in ((1, 0), (1, 1), (1, 2), (1, 3)):
+        def factors(pt, t):
+            picked = num[t][:].indirect(entries(n1_t, PARTS[pt]))
+            if pt == 1:
                 nc.scalar.activation(left[pt][:, t, :], picked, ACT.Copy)
                 root = sb.tile([P, widths[pt]], F32, name="root%d_%d" % (pt, t), tag="root%d_%d" % (pt, t), align_bytes=64)
                 nc.scalar.activation(root[:], den[pt, t][:], ACT.Abs_reciprocal_sqrt, bias=8.0)
@@ -193,14 +204,13 @@ def tile_picked_pqmixnorm2ebd_none_p_kernel(
                 ALU.mult,
             )
             nc.vector.quantize_mx(
-                out=z_w[:, spans[pt]].bitcast(FP8X4), scales=z_s[:, spans[pt]], in_=z_b[:].rearrange("p c t -> p (c t)")
+                out=z_w[:, PARTS[pt]].bitcast(FP8X4), scales=z_s[:, PARTS[pt]], in_=z_b[:].rearrange("p c t -> p (c t)")
             )
 
-        def second_product(m, w1q, w2q, span, tag, copy_out):
-            acc = ps.tile([P, span.stop - span.start], F32, name="h2_ps_" + tag, tag=tag)
-            cuts = [span.start, span.stop] if span.stop - span.start != 384 else [span.start, span.start + 256, span.stop]
+        def second_product(m, w1q, w2q, cuts, bank, copy_out):
+            acc = ps.tile([P, cuts[-1] - cuts[0]], F32, name="h2_ps_" + bank, tag=bank)
             for c0, c1 in zip(cuts, cuts[1:]):
-                dst = acc[:, c0 - span.start : c1 - span.start]
+                dst = acc[:, c0 - cuts[0] : c1 - cuts[0]]
                 nc.tensor.matmul_mx(
                     out=dst, lhsT=w2q[0][:].bitcast(FP8X4), lhsT_scale=w2q[1][:],
                     rhs=x2_w[:, c0:c1].bitcast(FP8X4), rhs_scale=x2_s[:, c0:c1], start=True, stop=False,
@@ -209,48 +219,49 @@ def tile_picked_pqmixnorm2ebd_none_p_kernel(
                     out=dst, lhsT=w1q[0][:].bitcast(FP8X4), lhsT_scale=w1q[1][:],
                     rhs=z_w[:, c0:c1].bitcast(FP8X4), rhs_scale=z_s[:, c0:c1], start=False, stop=True,
                 )
-            copy_out(h2[m][:, span], acc[:])
+            copy_out(h2[m][:, cuts[0] : cuts[-1]], acc[:])
 
-        LAG = 2
         steps = [(pt, t) for pt in range(2) for t in range(TILES)]
         for i in range(len(steps) + LAG):
             if i < TILES:
-                windows(i)
+                leave_psum(i)
             if i < len(steps):
-                fetch_far(*steps[i])
+                denominator(*steps[i])
             if i >= LAG:
                 pt, t = steps[i - LAG]
-                finish(pt, t)
+                factors(pt, t)
                 if t == TILES - 1:
                     if pt == 1:
                         nc.scalar.activation(warm[:, 2:3], right[1][:, TILES - 1, 0:1], ACT.Sigmoid)
                     quantise_z(pt)
-                    second_product(0, w1q0, w2q0, spans[pt], "b%d" % pt, (nc.scalar.copy, nc.vector.tensor_copy)[pt])
+                    second_product(0, w1q0, w2q0, PART_CUTS[pt], "b%d" % pt, (nc.scalar.copy, nc.vector.tensor_copy)[pt])
 
-        def gates(m, spans):
+        def gates(m, pieces):
             res = sb.tile([P, S], F32, name="res%d" % m)
             sg = sb.tile([P, S], F32, name="sg%d" % m)
             sg2 = sb.tile([P, S], F32, name="sgh%d" % m)
             dif = sb.tile([P, S], F32, name="dif%d" % m)
-            for span in spans:
-                window = h2[m][:].indirect(entries(n3_t, span))
+            for span in pieces:
+                looked_up = h2[m][:].indirect(entries(n3_t, span))
                 slope = prm[:, 0, m : m + 1]
-                nc.scalar.activation(sg[:, span], window, ACT.Sigmoid, bias=b_lo[:, m : m + 1], scale=slope)
-                nc.scalar.activation(sg2[:, span], window, ACT.Sigmoid, bias=b_hi[:, m : m + 1], scale=slope)
+                nc.scalar.activation(sg[:, span], looked_up, ACT.Sigmoid, bias=b_lo[:, m : m + 1], scale=slope)
+                nc.scalar.activation(sg2[:, span], looked_up, ACT.Sigmoid, bias=b_hi[:, m : m + 1], scale=slope)
                 nc.vector.tensor_tensor(dif[:, span], sg[:, span], sg2[:, span], ALU.subtract)
                 nc.vector.tensor_tensor(res[:, span], dif[:, span], h2[m][:, span], ALU.mult)
                 nc.sync.dma_start(out[blk(m), span], res[:, span])
 
-        whole = slice(0, S)
         for m in range(TILES):
             if m + 1 < TILES:
-                if m < 1:
-                    copy, tags = nc.scalar.copy, ("den0_1", "den0_2")
+                w2_name, w1_name = "w2_%d" % (m + 1), "w1_%d" % (m + 1)
+                if m == 0:
+                    copy, b_tags = nc.scalar.copy, ("den0_1", "den0_2")
+                    w_tags = ("den1_2", "den1_3")
                 else:
-                    copy, tags = nc.vector.tensor_copy, ("left1", "z_b1")
-                w2_b = round_weight(copy, w2_rest[:, :, blk(m)], "w2_%d" % (m + 1), tags[0])
-                w1_b = round_weight(copy, w1_rest[:, :, blk(m)], "w1_%d" % (m + 1), tags[1])
-                w2q = quantise_weight(w2_b, "w2_%d" % (m + 1))
-                w1q = quantise_weight(w1_b, "w1_%d" % (m + 1))
-                second_product(m + 1, w1q, w2q, whole, "a%d" % m, nc.vector.tensor_copy)
-            gates(m, [whole] if m + 1 < TILES else [slice(0, 256), slice(256, 384), slice(384, S)])
+                    copy, b_tags = nc.vector.tensor_copy, ("left1", "z_b1")
+                    w_tags = (w2_name + "_w", w1_name + "_w")
+                w2_b = round_weight(copy, w2_rest[:, :, blk(m)], w2_name, b_tags[0])
+                w1_b = round_weight(copy, w1_rest[:, :, blk(m)], w1_name, b_tags[1])
+                w2q = quantise_weight(w2_b, w2_name, w_tags[0])
+                w1q = quantise_weight(w1_b, w1_name, w_tags[1])
+                second_product(m + 1, w1q, w2q, ALL_CUTS, "a%d" % m, nc.vector.tensor_copy)
+            gates(m, [slice(0, S)] if m + 1 < TILES else LAST_PIECES)

from contextlib import ExitStack

import concourse.mybir as mybir

F32 = mybir.dt.float32
BF16 = mybir.dt.bfloat16
I32 = mybir.dt.int32
U32 = mybir.dt.uint32
U16 = mybir.dt.uint16
U8 = mybir.dt.uint8
FP8X4 = mybir.dt.float8_e4m3fn_x4
ACT = mybir.ActivationFunctionType
ALU = mybir.AluOpType

P = 128
T, S, N, G, H = 1024, 512, 512, 2048, 512
PACK = 4
TILES = 4
FLOPS = 3 * 2 * 512 * 512 * 512

PARTS = (slice(0, 384), slice(384, S))
PART_CUTS = ((0, 256, 384), (384, S))
ALL_CUTS = (0, S)
LAST_PIECES = (slice(0, 256), slice(256, 384), slice(384, S))
LAG = 2

OVERLAP = 64
AT_W2_REST = 0
AT_D_TAB = AT_W2_REST + PACK * (N - P) * 4 - OVERLAP
AT_XQ_W = AT_D_TAB + OVERLAP
AT_X2_W = AT_XQ_W + S * 4
AT_W1_REST = AT_D_TAB + G * 4 - OVERLAP
AT_W2_HEAD = AT_W1_REST + PACK * (N - P) * 4 + 2 * OVERLAP
AT_D_SG = AT_W2_HEAD + PACK * P * 4 - OVERLAP
AT_W1_HEAD = AT_D_SG + H - OVERLAP
AT_SIZE0 = AT_W2_HEAD + S * 2
AT_X_TAB = AT_W1_HEAD + PACK * P * 4


def tile_picked_pqmixnorm2ebd_none_p_kernel(
    tc, x_words, x_scales, d_words, d_scales, gn, w1, w2, sl, lo, hi, offs, k1, n1, n2, two, n3, out
):
    nc = tc.nc
    with ExitStack() as ctx:
        sb = ctx.enter_context(tc.tile_pool(name="sb", bufs=1))
        reuse = ctx.enter_context(tc.tile_pool(name="reuse", bufs=1))
        ps = ctx.enter_context(tc.psum_pool(name="ps", bufs=1))

        def load_list(src, name):
            lst = sb.tile([P, S // 16], U16, name=name)
            nc.sync.dma_start(lst[:], src)
            return lst

        def entries(lst, span):
            return lst[:, span.start // 16 : span.stop // 16]

        def blk(t):
            return slice(t * P, (t + 1) * P)

        warm = sb.tile([P, 3], F32, name="warm")
        nc.vector.memset(warm[:, 0:1], 1.0)
        nc.scalar.activation(warm[:, 1:2], warm[:, 0:1], ACT.Abs_reciprocal_sqrt)

        d_bytes = sb.tile([P, G], U8, name="d_bytes", align_bytes=64)
        nc.sync.dma_start(
            d_bytes[:].bitcast(I32),
            d_scales[0].bitcast(I32).unsqueeze(1).to_broadcast([16, 8, G // 4]),
        )
        k1_t = load_list(k1, "k1_t")
        offs_t = load_list(offs, "offs_t")
        x_bytes = sb.tile([P, T], U8, name="x_bytes", align_bytes=64)
        for q in range(4):
            nc.sync.dma_start(
                x_bytes[32 * q : 32 * q + 32, :].bitcast(I32),
                x_scales[0, 4 * q : 4 * q + 4, :].bitcast(I32).unsqueeze(0).to_broadcast([8, 4, T // 4]),
            )
        d_tab = reuse.tile([P, G], I32, name="d_tab", align_bytes=64, offset=AT_D_TAB)
        nc.sync.dma_start(d_tab[:], d_words[0].rearrange("p n t -> p (n t)").bitcast(I32))
        two_t = load_list(two, "two_t")
        x_tab = reuse.tile([P, T], I32, name="x_tab", align_bytes=64, offset=AT_X_TAB)
        nc.sync.dma_start(x_tab[:], x_words[0].rearrange("p n t -> p (n t)").bitcast(I32))
        n2_t = load_list(n2, "n2_t")
        n1_t = load_list(n1, "n1_t")
        n3_t = load_list(n3, "n3_t")
        gain = sb.tile([P, TILES], F32, name="gain")
        nc.gpsimd.dma_start(gain[:], gn.rearrange("(p t) o -> p (t o)", t=PACK))
        h2 = [sb.tile([P, 2 * S if m + 1 < TILES else S], F32, name="h2_%d" % m) for m in range(TILES)]

        d_sg = reuse.tile([P, H], U8, name="d_sg", align_bytes=64, offset=AT_D_SG)
        nc.vector.tensor_copy(d_sg[:], d_bytes[:].indirect(k1_t[:]))
        d_sc = sb.tile([P, H], U8, name="d_sc", tag="d_sc", align_bytes=64)
        nc.vector.tensor_copy(
            d_sc[:].rearrange("p (t m) -> p m t", t=PACK), d_sg[:].rearrange("p (m t) -> p m t", t=PACK)
        )
        for c in range(1, 4):
            nc.sync.dma_start(d_sc[c:P:32, :].bitcast(I32), d_sc[8 * c : P : 32, :].bitcast(I32))
        w2_rows = w2.rearrange("(p j) n -> p j n", j=PACK)
        w1_rows = w1.rearrange("(p j) n -> p j n", j=PACK)
        w2_head = reuse.tile([P, PACK, P], F32, name="w2_head", align_bytes=64, offset=AT_W2_HEAD)
        nc.sync.dma_start(w2_head[:], w2_rows[:, :, 0:P])
        w1_head = reuse.tile([P, PACK, P], F32, name="w1_head", align_bytes=64, offset=AT_W1_HEAD)
        nc.sync.dma_start(w1_head[:], w1_rows[:, :, 0:P])
        xq_s = sb.tile([P, S], U8, name="xq_s", align_bytes=64)
        nc.vector.tensor_copy(xq_s[:], x_bytes[:].indirect(offs_t[:]))
        d_wg = sb.tile([P, H], U32, name="d_wg", align_bytes=64)
        nc.vector.tensor_copy(d_wg[:], d_tab[:].bitcast(U32).indirect(k1_t[:]))
        d_w = sb.tile([P, H], U32, name="d_w", align_bytes=64)
        nc.vector.tensor_copy(
            d_w[:].rearrange("p (t m) -> p m t", t=PACK), d_wg[:].rearrange("p (m t) -> p m t", t=PACK)
        )
        xq_w = reuse.tile([P, S], U32, name="xq_w", align_bytes=64, offset=AT_XQ_W)
        nc.vector.tensor_copy(xq_w[:], x_tab[:].bitcast(U32).indirect(offs_t[:]))
        w2_rest = reuse.tile([P, PACK, N - P], F32, name="w2_rest", align_bytes=64, offset=AT_W2_REST)
        nc.sync.dma_start(w2_rest[:], w2_rows[:, :, P:N])
        w1_rest = reuse.tile([P, PACK, N - P], F32, name="w1_rest", align_bytes=64, offset=AT_W1_REST)
        nc.sync.dma_start(w1_rest[:], w1_rows[:, :, P:N])

        def round_weight(copy, raw, name, tag):
            grp = sb.tile([P, P, PACK], BF16, name=name + "_b", tag=tag, align_bytes=64)
            copy(grp[:].rearrange("p (c i) t -> p c t i", i=4), raw.rearrange("p t (c i) -> p c t i", i=4))
            return grp

        def quantise_weight(grp, name, tag):
            wq = sb.tile([P, P], U32, name=name + "_w", tag=tag, align_bytes=64)
            ws = sb.tile([P, P], U8, name=name + "_s", align_bytes=64)
            nc.vector.quantize_mx(out=wq[:].bitcast(FP8X4), scales=ws[:], in_=grp[:].rearrange("p c t -> p (c t)"))
            return wq, ws

        w2_b0 = round_weight(nc.scalar.copy, w2_head[:], "w2_0", "w2_0")
        w1_b0 = round_weight(nc.scalar.copy, w1_head[:], "w1_0", "w1_0")

        s_ps = []
        for t in range(TILES):
            acc = ps.tile([P, S], F32, name="s_ps%d" % t, tag="a%d" % t)
            nc.tensor.matmul_mx(
                out=acc[:], lhsT=d_w[:, blk(t)].bitcast(FP8X4), lhsT_scale=d_sc[:, blk(t)],
                rhs=xq_w[:].bitcast(FP8X4), rhs_scale=xq_s[:], start=True, stop=True,
            )
            s_ps.append(acc)

        x2_w = reuse.tile([P, S], U32, name="x2_w", align_bytes=64, offset=AT_X2_W)
        nc.vector.tensor_copy(x2_w[:], x_tab[:].bitcast(U32).indirect(two_t[:]))
        x2_s = reuse.tile([P, S], U8, name="x2_s", align_bytes=64, offset=AT_X_TAB)
        nc.vector.tensor_copy(x2_s[:], x_bytes[:].indirect(two_t[:]))
        w2q0 = quantise_weight(w2_b0, "w2_0", "w2_0_w")
        w1q0 = quantise_weight(w1_b0, "w1_0", "w1_0_w")

        prm = sb.tile([P, 3, 8], F32, name="prm", tag="d_sc", align_bytes=64)
        with nc.allow_non_contiguous_dma(reason="one value a partition and tile"):
            for i, vec in enumerate((sl, lo, hi)):
                nc.sync.dma_start(prm[:, i, 0:TILES], vec.rearrange("(t p) o -> p (t o)", t=TILES))
        neg_sl = sb.tile([P, TILES], F32, name="neg_sl")
        nc.gpsimd.tensor_scalar(neg_sl[:], prm[:, 0, 0:TILES], -1.0, 0.0, ALU.mult, ALU.add)
        b_lo = sb.tile([P, TILES], F32, name="b_lo")
        nc.gpsimd.tensor_tensor(b_lo[:], neg_sl[:], prm[:, 1, 0:TILES], ALU.mult)
        b_hi = sb.tile([P, TILES], F32, name="b_hi")
        nc.gpsimd.tensor_tensor(b_hi[:], neg_sl[:], prm[:, 2, 0:TILES], ALU.mult)

        size = [reuse.tile([P, S], F32, name="size0", align_bytes=64, offset=AT_SIZE0)]
        size.extend(sb.tile([P, S], F32, name="size%d" % t) for t in range(1, TILES))
        num = [sb.tile([P, S], F32, name="num%d" % t) for t in range(TILES)]
        widths = [span.stop - span.start for span in PARTS]
        left = [
            sb.tile([P, TILES, widths[pt]], F32, name="left%d" % pt, tag="left%d" % pt, align_bytes=64) for pt in range(2)
        ]
        right = [
            sb.tile([P, TILES, widths[pt]], F32, name="right%d" % pt, tag="right%d" % pt, align_bytes=64) for pt in range(2)
        ]
        den = {}
        last_far = sb.tile([P, S], F32, name="last_far")
        z_w = sb.tile([P, S], U32, name="z_w", align_bytes=64)
        z_s = sb.tile([P, S], U8, name="z_s", align_bytes=64)

        def leave_psum(t):
            nc.scalar.activation(size[t][:], s_ps[t][:], ACT.Abs)
            nc.vector.tensor_scalar(num[t][:], s_ps[t][:], gain[:, t : t + 1], None, ALU.mult)

        def denominator(pt, t):
            if t + 1 < TILES:
                far = h2[t][:, S + PARTS[pt].start : S + PARTS[pt].stop]
            else:
                far = last_far[:, PARTS[pt]]
            nc.scalar.activation(far, size[t][:].indirect(entries(n2_t, PARTS[pt])), ACT.Copy)
            den[pt, t] = sb.tile([P, widths[pt]], F32, name="den%d_%d" % (pt, t), tag="den%d_%d" % (pt, t), align_bytes=64)
            nc.vector.tensor_tensor(den[pt, t][:], far, size[t][:, PARTS[pt]], ALU.add)

        def factors(pt, t):
            picked = num[t][:].indirect(entries(n1_t, PARTS[pt]))
            if pt == 1:
                nc.scalar.activation(left[pt][:, t, :], picked, ACT.Copy)
                root = sb.tile([P, widths[pt]], F32, name="root%d_%d" % (pt, t), tag="root%d_%d" % (pt, t), align_bytes=64)
                nc.scalar.activation(root[:], den[pt, t][:], ACT.Abs_reciprocal_sqrt, bias=8.0)
                nc.scalar.activation(right[pt][:, t, :], root[:], ACT.Square)
            else:
                nc.scalar.activation(right[pt][:, t, :], den[pt, t][:], ACT.Abs_reciprocal_sqrt, bias=8.0)
                nc.vector.tensor_tensor(left[pt][:, t, :], picked, right[pt][:, t, :], ALU.mult)

        def quantise_z(pt):
            z_b = sb.tile([P, widths[pt], PACK], BF16, name="z_b%d" % pt, tag="z_b%d" % pt, align_bytes=64)
            nc.vector.tensor_tensor(
                z_b[:].rearrange("p (c i) t -> p c t i", i=4),
                left[pt][:].rearrange("p t (c i) -> p c t i", i=4),
                right[pt][:].rearrange("p t (c i) -> p c t i", i=4),
                ALU.mult,
            )
            nc.vector.quantize_mx(
                out=z_w[:, PARTS[pt]].bitcast(FP8X4), scales=z_s[:, PARTS[pt]], in_=z_b[:].rearrange("p c t -> p (c t)")
            )

        def second_product(m, w1q, w2q, cuts, bank, copy_out):
            acc = ps.tile([P, cuts[-1] - cuts[0]], F32, name="h2_ps_" + bank, tag=bank)
            for c0, c1 in zip(cuts, cuts[1:]):
                dst = acc[:, c0 - cuts[0] : c1 - cuts[0]]
                nc.tensor.matmul_mx(
                    out=dst, lhsT=w2q[0][:].bitcast(FP8X4), lhsT_scale=w2q[1][:],
                    rhs=x2_w[:, c0:c1].bitcast(FP8X4), rhs_scale=x2_s[:, c0:c1], start=True, stop=False,
                )
                nc.tensor.matmul_mx(
                    out=dst, lhsT=w1q[0][:].bitcast(FP8X4), lhsT_scale=w1q[1][:],
                    rhs=z_w[:, c0:c1].bitcast(FP8X4), rhs_scale=z_s[:, c0:c1], start=False, stop=True,
                )
            copy_out(h2[m][:, cuts[0] : cuts[-1]], acc[:])

        steps = [(pt, t) for pt in range(2) for t in range(TILES)]
        for i in range(len(steps) + LAG):
            if i < TILES:
                leave_psum(i)
            if i < len(steps):
                denominator(*steps[i])
            if i >= LAG:
                pt, t = steps[i - LAG]
                factors(pt, t)
                if t == TILES - 1:
                    if pt == 1:
                        nc.scalar.activation(warm[:, 2:3], right[1][:, TILES - 1, 0:1], ACT.Sigmoid)
                    quantise_z(pt)
                    second_product(0, w1q0, w2q0, PART_CUTS[pt], "b%d" % pt, (nc.scalar.copy, nc.vector.tensor_copy)[pt])

        def gates(m, pieces):
            res = sb.tile([P, S], F32, name="res%d" % m)
            sg = sb.tile([P, S], F32, name="sg%d" % m)
            sg2 = sb.tile([P, S], F32, name="sgh%d" % m)
            dif = sb.tile([P, S], F32, name="dif%d" % m)
            for span in pieces:
                looked_up = h2[m][:].indirect(entries(n3_t, span))
                slope = prm[:, 0, m : m + 1]
                nc.scalar.activation(sg[:, span], looked_up, ACT.Sigmoid, bias=b_lo[:, m : m + 1], scale=slope)
                nc.scalar.activation(sg2[:, span], looked_up, ACT.Sigmoid, bias=b_hi[:, m : m + 1], scale=slope)
                nc.vector.tensor_tensor(dif[:, span], sg[:, span], sg2[:, span], ALU.subtract)
                nc.vector.tensor_tensor(res[:, span], dif[:, span], h2[m][:, span], ALU.mult)
                nc.sync.dma_start(out[blk(m), span], res[:, span])

        for m in range(TILES):
            if m + 1 < TILES:
                w2_name, w1_name = "w2_%d" % (m + 1), "w1_%d" % (m + 1)
                if m == 0:
                    copy, b_tags = nc.scalar.copy, ("den0_1", "den0_2")
                    w_tags = ("den1_2", "den1_3")
                else:
                    copy, b_tags = nc.vector.tensor_copy, ("left1", "z_b1")
                    w_tags = (w2_name + "_w", w1_name + "_w")
                w2_b = round_weight(copy, w2_rest[:, :, blk(m)], w2_name, b_tags[0])
                w1_b = round_weight(copy, w1_rest[:, :, blk(m)], w1_name, b_tags[1])
                w2q = quantise_weight(w2_b, w2_name, w_tags[0])
                w1q = quantise_weight(w1_b, w1_name, w_tags[1])
                second_product(m + 1, w1q, w2q, ALL_CUTS, "a%d" % m, nc.vector.tensor_copy)
            gates(m, [slice(0, S)] if m + 1 < TILES else LAST_PIECES)
